import numpy as np
import ml_dtypes


def mxq(x, axis, fmt="e4m3"):
    dtype, down = {"e4m3": (ml_dtypes.float8_e4m3fn, 7), "e5m2": (ml_dtypes.float8_e5m2, 14)}[fmt]
    v = np.moveaxis(np.asarray(x, np.float32).astype(ml_dtypes.bfloat16).astype(np.float64), axis, -1)
    blocks = v.reshape(v.shape[:-1] + (-1, 32))
    amax = np.abs(blocks).max(-1, keepdims=True)
    byte = np.maximum(np.where(amax > 0, np.frexp(amax)[1] - 1 + 127, 0) - down, 1)
    scale = np.exp2(byte - 127.0)
    codes = (blocks / scale).astype(np.float32).astype(dtype).astype(np.float64)
    return np.moveaxis((codes * scale).reshape(v.shape), -1, axis)


WIDE = False


def mx_kscale(k):
    if not WIDE:
        return np.ones(k)
    levels = np.array([10, -10, 5, -5, 0])
    if k % 512:
        return np.exp2(np.random.permutation(np.resize(levels, k // 32))).repeat(32)
    a = np.empty((k // 512, 16))
    for p in range(k // 512):
        a[p, :8] = np.random.permutation(np.resize(levels, 8))
        for g in range(8):
            far = levels[np.abs(levels - a[p, g]) >= 10]
            a[p, g + 8] = far[np.random.randint(len(far))]
    return np.exp2(a.ravel()).repeat(32)


def f64(x):
    return np.asarray(x).astype(np.float64)


def striped(idx):
    return np.tile(idx.reshape(-1, 16).T, (8, 1)).astype(np.uint16)


def unstriped(offs):
    return offs[:16].T.reshape(-1).astype(np.int64)


def relu2(v):
    return np.maximum(v, 0.0) ** 2


K, T, D, S, V, N = 2048, 1024, 4, 1024, 256, 128


def setup_inputs():
    n = np.random.standard_normal
    s = mx_kscale(K)[:, None]
    return {
        "xT": (n((K, T)) * s).astype(np.float32),
        "w": (n((D, K, N)) / np.sqrt(D * K) / s[None]).astype(np.float32),
        "b": (0.3 * n((N, 1))).astype(np.float32),
        "gate": np.tile(np.random.uniform(0.2, 1.0, S), (N, 1)).astype(np.float32),
        "offs": striped(np.random.permutation(T)[:S]),
    }


def reference(xT, w, b, gate, offs):
    idx = unstriped(offs)
    xq = mxq(f64(xT)[:, idx], 0, "e4m3")
    wq = mxq(f64(w), 1, "e4m3")
    y = sum(wq[d].T @ xq[:, d * V:(d + 1) * V] for d in range(D))
    y = relu2(y + f64(b))
    out = np.zeros((N, T))
    out[:, idx] = f64(gate) * np.tile(y, (1, D))
    return out

@@ -1,0 +1,160 @@
+from contextlib import ExitStack
+
+import concourse.mybir as mybir
+
+K, T, D, S, V, N = 2048, 1024, 4, 1024, 256, 128
+FLOPS = 2 * N * S * K
+
+F32 = mybir.dt.float32
+BF16 = mybir.dt.bfloat16
+U32 = mybir.dt.uint32
+U16 = mybir.dt.uint16
+U8 = mybir.dt.uint8
+FP8X4 = mybir.dt.float8_e4m3fn_x4
+ACT = mybir.ActivationFunctionType
+ALU = mybir.AluOpType
+
+P = 128
+PACK = 4
+PASS_K = P * PACK
+PASSES = K // PASS_K
+CHUNK = 256
+CHUNKS = T // CHUNK
+
+
+def tile_picked_tome_lin_relu2_sub_e_kernel(tc, xT, w, b, gate, offs, out):
+    nc = tc.nc
+    with ExitStack() as ctx:
+        keep = ctx.enter_context(tc.tile_pool(name="keep", bufs=1))
+        psum = ctx.enter_context(tc.psum_pool(name="psum", bufs=1))
+
+        offsets = keep.tile([P, S // 16], U16, name="offsets")
+        bias = keep.tile([P, 1], F32, name="bias")
+        gates = keep.tile([P, S], F32, name="gates")
+        x_raw = [keep.tile([P, PACK, T], F32, name=f"x_raw{a}") for a in range(PASSES)]
+        w_raw = [keep.tile([P, D, PACK, N], F32, name=f"w_raw{a}") for a in range(PASSES)]
+        x_bf = [[keep.tile([P, CHUNK, PACK], BF16, name=f"x_bf{a}_{c}", align_bytes=64) for c in range(CHUNKS)] for a in range(PASSES)]
+        w_bf = [keep.tile([P, D, N, PACK], BF16, name=f"w_bf{a}", align_bytes=64) for a in range(PASSES)]
+        x_codes = [keep.tile([P, T], U32, name=f"x_codes{a}", align_bytes=64) for a in range(PASSES)]
+        x_scales = keep.tile([P, T], U8, name="x_scales", align_bytes=64)
+        picked_codes = [keep.tile([P, S], U32, name=f"picked_codes{a}", align_bytes=64) for a in range(PASSES)]
+        picked_scales = keep.tile([P, S], U8, name="picked_scales", align_bytes=64)
+        w_codes = [keep.tile([P, D * N], U32, name=f"w_codes{a}", align_bytes=64) for a in range(PASSES)]
+        w_scales = [keep.tile([P, D * N], U8, name=f"w_scales{a}", align_bytes=64) for a in range(PASSES)]
+        r = keep.tile([P, V], F32, name="r")
+        y = keep.tile([P, V], F32, name="y")
+        result = keep.tile([P, T], F32, name="result")
+        acc = psum.tile([P, V], F32, name="acc")
+
+        def load_x(a):
+            nc.sync.dma_start(out=x_raw[a][:], in_=xT[a * PASS_K : (a + 1) * PASS_K, :].rearrange("(p j) t -> p j t", j=PACK))
+
+        def load_w(a, d0, d1):
+            src = w[d0:d1, a * PASS_K : (a + 1) * PASS_K, :].rearrange("d (p j) m -> p d j m", j=PACK)
+            nc.sync.dma_start(out=w_raw[a][:, d0:d1, :, :], in_=src)
+
+        nc.scalar.dma_start(out=bias[:], in_=b)
+        load_w(0, 0, 2)
+        load_w(0, 2, 4)
+        nc.sync.dma_start(offsets[:], offs)
+        for a in range(PASSES):
+            load_x(a)
+        load_w(1, 0, 4)
+        load_w(2, 0, 4)
+        load_w(3, 0, 2)
+        load_w(3, 2, 4)
+        for h in range(2):
+            nc.sync.dma_start(out=gates[:, h * 512 : (h + 1) * 512], in_=gate[:, h * 512 : (h + 1) * 512])
+
+        nc.gpsimd.memset(x_scales[:], 0)
+
+        def interleave(engine, dst, src):
+            o = dst.rearrange("p (c i) j -> p c j i", i=4)
+            s = src.rearrange("p j (c i) -> p c j i", i=4)
+            if engine == "v":
+                nc.vector.tensor_copy(out=o, in_=s)
+            else:
+                nc.scalar.copy(out=o, in_=s)
+
+        def cast_x(engine, a, c):
+            interleave(engine, x_bf[a][c][:], x_raw[a][:, :, c * CHUNK : (c + 1) * CHUNK])
+
+        def cast_w(engine, a, d):
+            interleave(engine, w_bf[a][:, d, :, :], w_raw[a][:, d, :, :])
+
+        def quantize_x(a, c):
+            cols = slice(c * CHUNK, (c + 1) * CHUNK)
+            nc.vector.quantize_mx(
+                out=x_codes[a][:, cols].bitcast(FP8X4),
+                scales=x_scales[4 * a : P, cols],
+                in_=x_bf[a][c][:].rearrange("p t j -> p (t j)"),
+            )
+
+        def quantize_w(a, d0, d1):
+            cols = slice(d0 * N, d1 * N)
+            nc.vector.quantize_mx(
+                out=w_codes[a][:, cols].bitcast(FP8X4),
+                scales=w_scales[a][:, cols],
+                in_=w_bf[a][:, d0:d1, :, :].rearrange("p d m j -> p (d m j)"),
+            )
+
+        def gather(dst, src, h):
+            nc.vector.tensor_copy(dst[:, h * 512 : (h + 1) * 512], src[:].indirect(offsets[:, h * 32 : (h + 1) * 32]))
+
+        def gather_words(a):
+            for h in range(2):
+                gather(picked_codes[a], x_codes[a], h)
+
+        def multiply(a, d):
+            nc.tensor.matmul_mx(
+                out=acc[:],
+                lhsT=w_codes[a][:, d * N : (d + 1) * N].bitcast(FP8X4),
+                lhsT_scale=w_scales[a][:, d * N : (d + 1) * N],
+                rhs=picked_codes[a][:, d * V : (d + 1) * V].bitcast(FP8X4),
+                rhs_scale=picked_scales[4 * a : P, d * V : (d + 1) * V],
+                start=(a == 0 and d == 0),
+                stop=(a == PASSES - 1 and d == D - 1),
+            )
+
+        for d in range(D):
+            cast_w("vs"[d % 2], 0, d)
+        quantize_w(0, 0, 4)
+
+        for a in range(PASSES):
+            engines = "sssv" if a < 3 else "svvv"
+            for c in range(CHUNKS):
+                cast_x(engines[c], a, c)
+            if a > 0:
+                gather_words(a - 1)
+            for c in range(CHUNKS):
+                quantize_x(a, c)
+
+        for d in range(D):
+            cast_w("s", 1, d)
+        for h in range(2):
+            gather(picked_scales, x_scales, h)
+        quantize_w(1, 0, 4)
+        gather_words(3)
+        for d in range(D):
+            cast_w("s", 2, d)
+        quantize_w(2, 0, 4)
+        for a in range(3):
+            for d in range(D):
+                multiply(a, d)
+        for d0 in (0, 2):
+            cast_w("s", 3, d0)
+            cast_w("v", 3, d0 + 1)
+            quantize_w(3, d0, d0 + 2)
+            multiply(3, d0)
+            multiply(3, d0 + 1)
+
+        nc.scalar.activation(out=r[:], in_=acc[:], func=ACT.Relu, bias=bias[:, 0:1])
+        nc.scalar.activation(out=y[:], in_=r[:], func=ACT.Square)
+        for d in range(D):
+            nc.vector.tensor_tensor(
+                result[:].indirect(offsets[:, d * 16 : (d + 1) * 16]),
+                y[:],
+                gates[:, d * V : (d + 1) * V],
+                ALU.mult,
+            )
+        nc.sync.dma_start(out=out, in_=result[:])

@@ -18,8 +18,13 @@ P = 128
 PACK = 4
 PASS_K = P * PACK
 PASSES = K // PASS_K
+HALF = T // 2
 CHUNK = 256
 CHUNKS = T // CHUNK
+VH = V // 2
+
+X_ENGINES = ("SVSV", "SSSV", "SSSV", "SSSV")
+W_ENGINES = ("SSSV", "SSSV", "SSSV", "SVSV")
 
 
 def tile_picked_tome_lin_relu2_sub_e_kernel(tc, xT, w, b, gate, offs, out):
@@ -30,9 +35,9 @@ def tile_picked_tome_lin_relu2_sub_e_kernel(tc, xT, w, b, gate, offs, out):
 
         offsets = keep.tile([P, S // 16], U16, name="offsets")
         bias = keep.tile([P, 1], F32, name="bias")
-        gates = keep.tile([P, S], F32, name="gates")
-        x_raw = [keep.tile([P, PACK, T], F32, name=f"x_raw{a}") for a in range(PASSES)]
-        w_raw = [keep.tile([P, D, PACK, N], F32, name=f"w_raw{a}") for a in range(PASSES)]
+        gates = [keep.tile([P, S // 2], F32, name=f"gates{h}") for h in range(2)]
+        x_raw = [[keep.tile([P, PACK, HALF], F32, name=f"x_raw{a}_{h}") for h in range(2)] for a in range(PASSES)]
+        w_raw = [[keep.tile([P, 2, PACK, N], F32, name=f"w_raw{a}_{i}") for i in range(2)] for a in range(PASSES)]
         x_bf = [[keep.tile([P, CHUNK, PACK], BF16, name=f"x_bf{a}_{c}", align_bytes=64) for c in range(CHUNKS)] for a in range(PASSES)]
         w_bf = [keep.tile([P, D, N, PACK], BF16, name=f"w_bf{a}", align_bytes=64) for a in range(PASSES)]
         x_codes = [keep.tile([P, T], U32, name=f"x_codes{a}", align_bytes=64) for a in range(PASSES)]
@@ -41,46 +46,47 @@ def tile_picked_tome_lin_relu2_sub_e_kernel(tc, xT, w, b, gate, offs, out):
         picked_scales = keep.tile([P, S], U8, name="picked_scales", align_bytes=64)
         w_codes = [keep.tile([P, D * N], U32, name=f"w_codes{a}", align_bytes=64) for a in range(PASSES)]
         w_scales = [keep.tile([P, D * N], U8, name=f"w_scales{a}", align_bytes=64) for a in range(PASSES)]
-        r = keep.tile([P, V], F32, name="r")
-        y = keep.tile([P, V], F32, name="y")
+        r = [keep.tile([P, VH], F32, name=f"r{h}") for h in range(2)]
+        y = keep.tile([P, 2, V], F32, name="y")
         result = keep.tile([P, T], F32, name="result")
-        acc = psum.tile([P, V], F32, name="acc")
+        acc = [psum.tile([P, VH], F32, name=f"acc{h}") for h in range(2)]
 
-        def load_x(a):
-            nc.sync.dma_start(out=x_raw[a][:], in_=xT[a * PASS_K : (a + 1) * PASS_K, :].rearrange("(p j) t -> p j t", j=PACK))
+        def load_x(a, h):
+            src = xT[a * PASS_K : (a + 1) * PASS_K, h * HALF : (h + 1) * HALF]
+            nc.sync.dma_start(out=x_raw[a][h][:], in_=src.rearrange("(p j) t -> p j t", j=PACK))
 
-        def load_w(a, d0, d1):
-            src = w[d0:d1, a * PASS_K : (a + 1) * PASS_K, :].rearrange("d (p j) m -> p d j m", j=PACK)
-            nc.sync.dma_start(out=w_raw[a][:, d0:d1, :, :], in_=src)
+        def load_w(a, i):
+            src = w[2 * i : 2 * i + 2, a * PASS_K : (a + 1) * PASS_K, :].rearrange("d (p j) m -> p d j m", j=PACK)
+            nc.sync.dma_start(out=w_raw[a][i][:], in_=src)
 
         nc.scalar.dma_start(out=bias[:], in_=b)
-        load_w(0, 0, 2)
-        load_w(0, 2, 4)
-        nc.sync.dma_start(offsets[:], offs)
         for a in range(PASSES):
-            load_x(a)
-        load_w(1, 0, 4)
-        load_w(2, 0, 4)
-        load_w(3, 0, 2)
-        load_w(3, 2, 4)
+            for h in range(2):
+                load_x(a, h)
+            if a == 0:
+                nc.sync.dma_start(offsets[:], offs)
+        for a in range(PASSES):
+            for i in range(2):
+                load_w(a, i)
         for h in range(2):
-            nc.sync.dma_start(out=gates[:, h * 512 : (h + 1) * 512], in_=gate[:, h * 512 : (h + 1) * 512])
+            nc.sync.dma_start(out=gates[h][:], in_=gate[:, h * 512 : (h + 1) * 512])
 
         nc.gpsimd.memset(x_scales[:], 0)
 
         def interleave(engine, dst, src):
             o = dst.rearrange("p (c i) j -> p c j i", i=4)
             s = src.rearrange("p j (c i) -> p c j i", i=4)
-            if engine == "v":
+            if engine == "V":
                 nc.vector.tensor_copy(out=o, in_=s)
             else:
                 nc.scalar.copy(out=o, in_=s)
 
-        def cast_x(engine, a, c):
-            interleave(engine, x_bf[a][c][:], x_raw[a][:, :, c * CHUNK : (c + 1) * CHUNK])
+        def cast_x(a, c):
+            lo = (c % 2) * CHUNK
+            interleave(X_ENGINES[a][c], x_bf[a][c][:], x_raw[a][c // 2][:, :, lo : lo + CHUNK])
 
-        def cast_w(engine, a, d):
-            interleave(engine, w_bf[a][:, d, :, :], w_raw[a][:, d, :, :])
+        def cast_w(a, d):
+            interleave(W_ENGINES[a][d], w_bf[a][:, d, :, :], w_raw[a][d // 2][:, d % 2, :, :])
 
         def quantize_x(a, c):
             cols = slice(c * CHUNK, (c + 1) * CHUNK)
@@ -106,55 +112,57 @@ def tile_picked_tome_lin_relu2_sub_e_kernel(tc, xT, w, b, gate, offs, out):
                 gather(picked_codes[a], x_codes[a], h)
 
         def multiply(a, d):
-            nc.tensor.matmul_mx(
-                out=acc[:],
-                lhsT=w_codes[a][:, d * N : (d + 1) * N].bitcast(FP8X4),
-                lhsT_scale=w_scales[a][:, d * N : (d + 1) * N],
-                rhs=picked_codes[a][:, d * V : (d + 1) * V].bitcast(FP8X4),
-                rhs_scale=picked_scales[4 * a : P, d * V : (d + 1) * V],
-                start=(a == 0 and d == 0),
-                stop=(a == PASSES - 1 and d == D - 1),
-            )
-
-        for d in range(D):
-            cast_w("vs"[d % 2], 0, d)
-        quantize_w(0, 0, 4)
+            for h in range(2):
+                cols = slice(d * V + h * VH, d * V + (h + 1) * VH)
+                nc.tensor.matmul_mx(
+                    out=acc[h][:],
+                    lhsT=w_codes[a][:, d * N : (d + 1) * N].bitcast(FP8X4),
+                    lhsT_scale=w_scales[a][:, d * N : (d + 1) * N],
+                    rhs=picked_codes[a][:, cols].bitcast(FP8X4),
+                    rhs_scale=picked_scales[4 * a : P, cols],
+                    start=(a == 0 and d == 0),
+                    stop=(a == PASSES - 1 and d == D - 1),
+                )
 
         for a in range(PASSES):
-            engines = "sssv" if a < 3 else "svvv"
             for c in range(CHUNKS):
-                cast_x(engines[c], a, c)
-            if a > 0:
-                gather_words(a - 1)
+                cast_x(a, c)
             for c in range(CHUNKS):
                 quantize_x(a, c)
+            if a < PASSES - 1:
+                gather_words(a)
 
-        for d in range(D):
-            cast_w("s", 1, d)
         for h in range(2):
             gather(picked_scales, x_scales, h)
-        quantize_w(1, 0, 4)
-        gather_words(3)
         for d in range(D):
-            cast_w("s", 2, d)
-        quantize_w(2, 0, 4)
-        for a in range(3):
+            cast_w(0, d)
+        quantize_w(0, 0, 4)
+        for d in range(D):
+            multiply(0, d)
+        gather_words(3)
+        for a in (1, 2):
+            for d in range(D):
+                cast_w(a, d)
+            quantize_w(a, 0, 4)
             for d in range(D):
                 multiply(a, d)
         for d0 in (0, 2):
-            cast_w("s", 3, d0)
-            cast_w("v", 3, d0 + 1)
+            cast_w(3, d0)
+            cast_w(3, d0 + 1)
             quantize_w(3, d0, d0 + 2)
             multiply(3, d0)
             multiply(3, d0 + 1)
 
-        nc.scalar.activation(out=r[:], in_=acc[:], func=ACT.Relu, bias=bias[:, 0:1])
-        nc.scalar.activation(out=y[:], in_=r[:], func=ACT.Square)
-        for d in range(D):
+        r_twice = [r[h][:].unsqueeze(1).to_broadcast([P, 2, VH]) for h in range(2)]
+        nc.scalar.activation(out=r[0][:], in_=acc[0][:], func=ACT.Relu, bias=bias[:, 0:1])
+        nc.vector.tensor_scalar(out=r[1][:], in0=acc[1][:], scalar1=bias[:, 0:1], scalar2=0.0, op0=ALU.add, op1=ALU.max)
+        nc.scalar.activation(out=y[:, :, 0:VH], in_=r_twice[0], func=ACT.Square)
+        nc.vector.tensor_tensor(out=y[:, :, VH:V], in0=r_twice[1], in1=r_twice[1], op=ALU.mult)
+        for h in range(2):
             nc.vector.tensor_tensor(
-                result[:].indirect(offsets[:, d * 16 : (d + 1) * 16]),
-                y[:],
-                gates[:, d * V : (d + 1) * V],
+                result[:].indirect(offsets[:, 32 * h : 32 * (h + 1)]),
+                y[:].rearrange("p q v -> p (q v)"),
+                gates[h][:],
                 ALU.mult,
             )
         nc.sync.dma_start(out=out, in_=result[:])

@@ -158,11 +158,9 @@ def tile_picked_tome_lin_relu2_sub_e_kernel(tc, xT, w, b, gate, offs, out):
         nc.vector.tensor_scalar(out=r[1][:], in0=acc[1][:], scalar1=bias[:, 0:1], scalar2=0.0, op0=ALU.add, op1=ALU.max)
         nc.scalar.activation(out=y[:, :, 0:VH], in_=r_twice[0], func=ACT.Square)
         nc.vector.tensor_tensor(out=y[:, :, VH:V], in0=r_twice[1], in1=r_twice[1], op=ALU.mult)
+        gated = [keep.tile([P, S // 2], F32, name=f"gated{h}") for h in range(2)]
         for h in range(2):
-            nc.vector.tensor_tensor(
-                result[:].indirect(offsets[:, 32 * h : 32 * (h + 1)]),
-                y[:].rearrange("p q v -> p (q v)"),
-                gates[h][:],
-                ALU.mult,
-            )
+            nc.vector.tensor_tensor(out=gated[h][:], in0=y[:].rearrange("p q v -> p (q v)"), in1=gates[h][:], op=ALU.mult)
+        for h in range(2):
+            nc.vector.tensor_copy(result[:].indirect(offsets[:, 32 * h : 32 * (h + 1)]), gated[h][:])
         nc.sync.dma_start(out=out, in_=result[:])

@@ -19,12 +19,14 @@ PACK = 4
 PASS_K = P * PACK
 PASSES = K // PASS_K
 HALF = T // 2
-CHUNK = 256
-CHUNKS = T // CHUNK
+X_WINDOW = 1408
+OUT_WINDOW = 2048
 VH = V // 2
 
-X_ENGINES = ("SVSV", "SSSV", "SSSV", "SSSV")
-W_ENGINES = ("SSSV", "SSSV", "SSSV", "SVSV")
+X_VECTOR = ((192, 320), (0, 256), (320, 192), (64, 64))
+W_ENGINES = ("SSSS", "SSSS", "VSSS", "SVSB")
+X_SPLIT = ((512, 512), (512, 512), (1024,), (512, 512))
+W3_GROUPS = [(0, 1), (2,), (3,)]
 
 
 def tile_picked_tome_lin_relu2_sub_e_kernel(tc, xT, w, b, gate, offs, out):
@@ -35,43 +37,42 @@ def tile_picked_tome_lin_relu2_sub_e_kernel(tc, xT, w, b, gate, offs, out):
 
         offsets = keep.tile([P, S // 16], U16, name="offsets")
         bias = keep.tile([P, 1], F32, name="bias")
-        gates = [keep.tile([P, S // 2], F32, name=f"gates{h}") for h in range(2)]
-        x_raw = [[keep.tile([P, PACK, HALF], F32, name=f"x_raw{a}_{h}") for h in range(2)] for a in range(PASSES)]
-        w_raw = [[keep.tile([P, 2, PACK, N], F32, name=f"w_raw{a}_{i}") for i in range(2)] for a in range(PASSES)]
-        x_bf = [[keep.tile([P, CHUNK, PACK], BF16, name=f"x_bf{a}_{c}", align_bytes=64) for c in range(CHUNKS)] for a in range(PASSES)]
-        w_bf = [keep.tile([P, D, N, PACK], BF16, name=f"w_bf{a}", align_bytes=64) for a in range(PASSES)]
-        x_codes = [keep.tile([P, T], U32, name=f"x_codes{a}", align_bytes=64) for a in range(PASSES)]
-        x_scales = keep.tile([P, T], U8, name="x_scales", align_bytes=64)
-        picked_codes = [keep.tile([P, S], U32, name=f"picked_codes{a}", align_bytes=64) for a in range(PASSES)]
+        gates = keep.tile([P, S], F32, name="gates")
+        x_raw = [[keep.tile([P, PACK, n], F32, name=f"x_raw{a}_{i}") for i, n in enumerate(X_SPLIT[a])] for a in range(PASSES)]
+        w_groups = [[(0, 1, 2, 3)]] * 3 + [W3_GROUPS]
+        w_raw = [[keep.tile([P, len(g), PACK, N], F32, name=f"w_raw{a}_{i}") for i, g in enumerate(w_groups[a])] for a in range(PASSES)]
+        x_bf = [[keep.tile([P, HALF, PACK], BF16, name=f"x_bf{a}_{c}", align_bytes=64) for c in range(2)] for a in range(PASSES)]
+        w_bf = [keep.tile([P, D, N, PACK], BF16, name=f"w_bf{a}", tag=f"ring{a}", align_bytes=64) for a in range(PASSES)]
+        x_codes = [keep.tile([P, X_WINDOW], U32, name=f"x_codes{a}", align_bytes=64) for a in range(PASSES)]
+        x_scales = keep.tile([P, X_WINDOW], U8, name="x_scales", align_bytes=64)
+        picked_codes = [keep.tile([P, S], U32, name=f"picked_codes{a}", align_bytes=64) for a in range(PASSES - 1)]
         picked_scales = keep.tile([P, S], U8, name="picked_scales", align_bytes=64)
         w_codes = [keep.tile([P, D * N], U32, name=f"w_codes{a}", align_bytes=64) for a in range(PASSES)]
         w_scales = [keep.tile([P, D * N], U8, name=f"w_scales{a}", align_bytes=64) for a in range(PASSES)]
-        r = [keep.tile([P, VH], F32, name=f"r{h}") for h in range(2)]
-        y = keep.tile([P, 2, V], F32, name="y")
-        result = keep.tile([P, T], F32, name="result")
+        r = keep.tile([P, V], F32, name="r")
+        ug = keep.tile([P, V], F32, name="ug")
+        y = keep.tile([P, D - 1, V], F32, name="y")
+        result = keep.tile([P, OUT_WINDOW], F32, name="result")
         acc = [psum.tile([P, VH], F32, name=f"acc{h}") for h in range(2)]
-
-        def load_x(a, h):
-            src = xT[a * PASS_K : (a + 1) * PASS_K, h * HALF : (h + 1) * HALF]
-            nc.sync.dma_start(out=x_raw[a][h][:], in_=src.rearrange("(p j) t -> p j t", j=PACK))
-
-        def load_w(a, i):
-            src = w[2 * i : 2 * i + 2, a * PASS_K : (a + 1) * PASS_K, :].rearrange("d (p j) m -> p d j m", j=PACK)
-            nc.sync.dma_start(out=w_raw[a][i][:], in_=src)
 
         nc.scalar.dma_start(out=bias[:], in_=b)
         for a in range(PASSES):
-            for h in range(2):
-                load_x(a, h)
+            t0 = 0
+            for i, n in enumerate(X_SPLIT[a]):
+                src = xT[a * PASS_K : (a + 1) * PASS_K, t0 : t0 + n]
+                nc.sync.dma_start(out=x_raw[a][i][:], in_=src.rearrange("(p j) t -> p j t", j=PACK))
+                t0 += n
             if a == 0:
                 nc.sync.dma_start(offsets[:], offs)
         for a in range(PASSES):
-            for i in range(2):
-                load_w(a, i)
-        for h in range(2):
-            nc.sync.dma_start(out=gates[h][:], in_=gate[:, h * 512 : (h + 1) * 512])
+            for i, g in enumerate(w_groups[a]):
+                src = w[g[0] : g[-1] + 1, a * PASS_K : (a + 1) * PASS_K, :].rearrange("d (p j) m -> p d j m", j=PACK)
+                nc.sync.dma_start(out=w_raw[a][i][:], in_=src)
+        nc.sync.dma_start(out=gates[:], in_=gate)
 
         nc.gpsimd.memset(x_scales[:], 0)
+        for a in range(PASSES):
+            nc.gpsimd.memset(x_codes[a][:, T:X_WINDOW], 0)
 
         def interleave(engine, dst, src):
             o = dst.rearrange("p (c i) j -> p c j i", i=4)
@@ -81,86 +82,111 @@ def tile_picked_tome_lin_relu2_sub_e_kernel(tc, xT, w, b, gate, offs, out):
             else:
                 nc.scalar.copy(out=o, in_=s)
 
-        def cast_x(a, c):
-            lo = (c % 2) * CHUNK
-            interleave(X_ENGINES[a][c], x_bf[a][c][:], x_raw[a][c // 2][:, :, lo : lo + CHUNK])
+        def x_columns(a, lo, hi):
+            t0 = 0
+            for i, n in enumerate(X_SPLIT[a]):
+                if t0 <= lo and hi <= t0 + n:
+                    return x_raw[a][i][:, :, lo - t0 : hi - t0]
+                t0 += n
 
-        def cast_w(a, d):
-            interleave(W_ENGINES[a][d], w_bf[a][:, d, :, :], w_raw[a][d // 2][:, d % 2, :, :])
+        def convert_x(a, c):
+            lo, mid, hi = c * HALF, (c + 1) * HALF - X_VECTOR[a][c], (c + 1) * HALF
+            if mid > lo:
+                interleave("S", x_bf[a][c][:, 0 : mid - lo, :], x_columns(a, lo, mid))
+            if hi > mid:
+                interleave("V", x_bf[a][c][:, mid - lo : HALF, :], x_columns(a, mid, hi))
 
         def quantize_x(a, c):
-            cols = slice(c * CHUNK, (c + 1) * CHUNK)
+            cols = slice(c * HALF, (c + 1) * HALF)
             nc.vector.quantize_mx(
                 out=x_codes[a][:, cols].bitcast(FP8X4),
                 scales=x_scales[4 * a : P, cols],
                 in_=x_bf[a][c][:].rearrange("p t j -> p (t j)"),
             )
 
-        def quantize_w(a, d0, d1):
-            cols = slice(d0 * N, d1 * N)
+        def convert_w(a, i):
+            for n, d in enumerate(w_groups[a][i]):
+                e = W_ENGINES[a][d]
+                if e == "B":
+                    interleave("S", w_bf[a][:, d, 0 : N // 2, :], w_raw[a][i][:, n, :, 0 : N // 2])
+                    interleave("V", w_bf[a][:, d, N // 2 : N, :], w_raw[a][i][:, n, :, N // 2 : N])
+                else:
+                    interleave(e, w_bf[a][:, d, :, :], w_raw[a][i][:, n, :, :])
+
+        def quantize_w(a, i):
+            g = w_groups[a][i]
+            cols = slice(g[0] * N, (g[-1] + 1) * N)
             nc.vector.quantize_mx(
                 out=w_codes[a][:, cols].bitcast(FP8X4),
                 scales=w_scales[a][:, cols],
-                in_=w_bf[a][:, d0:d1, :, :].rearrange("p d m j -> p (d m j)"),
+                in_=w_bf[a][:, g[0] : g[-1] + 1, :, :].rearrange("p d m j -> p (d m j)"),
             )
 
-        def gather(dst, src, h):
-            nc.vector.tensor_copy(dst[:, h * 512 : (h + 1) * 512], src[:].indirect(offsets[:, h * 32 : (h + 1) * 32]))
-
-        def gather_words(a):
-            for h in range(2):
-                gather(picked_codes[a], x_codes[a], h)
+        def gather(dst, src, lo, hi):
+            nc.vector.tensor_copy(dst, src[:].indirect(offsets[:, lo // 16 : hi // 16]))
 
         def multiply(a, d):
             for h in range(2):
                 cols = slice(d * V + h * VH, d * V + (h + 1) * VH)
+                if a < PASSES - 1:
+                    codes = picked_codes[a][:, cols]
+                else:
+                    codes = last_codes[d // 2][:, cols.start % (S // 2) : cols.start % (S // 2) + VH]
                 nc.tensor.matmul_mx(
                     out=acc[h][:],
                     lhsT=w_codes[a][:, d * N : (d + 1) * N].bitcast(FP8X4),
                     lhsT_scale=w_scales[a][:, d * N : (d + 1) * N],
-                    rhs=picked_codes[a][:, cols].bitcast(FP8X4),
+                    rhs=codes.bitcast(FP8X4),
                     rhs_scale=picked_scales[4 * a : P, cols],
                     start=(a == 0 and d == 0),
                     stop=(a == PASSES - 1 and d == D - 1),
                 )
 
+        def weights(a, i):
+            convert_w(a, i)
+            quantize_w(a, i)
+
         for a in range(PASSES):
-            for c in range(CHUNKS):
-                cast_x(a, c)
-            for c in range(CHUNKS):
+            for c in range(2):
+                convert_x(a, c)
+            for c in range(2):
                 quantize_x(a, c)
             if a < PASSES - 1:
-                gather_words(a)
-
-        for h in range(2):
-            gather(picked_scales, x_scales, h)
-        for d in range(D):
-            cast_w(0, d)
-        quantize_w(0, 0, 4)
-        for d in range(D):
+                gather(picked_codes[a][:], x_codes[a], 0, S)
+        gather(picked_scales[:, 0 : S // 2], x_scales, 0, S // 2)
+        weights(0, 0)
+        gather(picked_scales[:, S // 2 : S], x_scales, S // 2, S)
+        for d in (0, 1):
             multiply(0, d)
-        gather_words(3)
-        for a in (1, 2):
-            for d in range(D):
-                cast_w(a, d)
-            quantize_w(a, 0, 4)
-            for d in range(D):
+        last_codes = []
+        last_codes.append(keep.tile([P, S // 2], U32, name="last_codes0", tag="ring0", align_bytes=64))
+        gather(last_codes[0][:], x_codes[3], 0, S // 2)
+        weights(1, 0)
+        for d in (0, 1):
+            multiply(1, d)
+        for a in (0, 1):
+            for d in (2, 3):
                 multiply(a, d)
-        for d0 in (0, 2):
-            cast_w(3, d0)
-            cast_w(3, d0 + 1)
-            quantize_w(3, d0, d0 + 2)
-            multiply(3, d0)
-            multiply(3, d0 + 1)
+        last_codes.append(keep.tile([P, S // 2], U32, name="last_codes1", tag="ring1", align_bytes=64))
+        gather(last_codes[1][:], x_codes[3], S // 2, S)
+        weights(2, 0)
+        for d in range(D):
+            multiply(2, d)
+        for i, g in enumerate(W3_GROUPS):
+            weights(3, i)
+            for d in g:
+                multiply(3, d)
 
-        r_twice = [r[h][:].unsqueeze(1).to_broadcast([P, 2, VH]) for h in range(2)]
-        nc.scalar.activation(out=r[0][:], in_=acc[0][:], func=ACT.Relu, bias=bias[:, 0:1])
-        nc.vector.tensor_scalar(out=r[1][:], in0=acc[1][:], scalar1=bias[:, 0:1], scalar2=0.0, op0=ALU.add, op1=ALU.max)
-        nc.scalar.activation(out=y[:, :, 0:VH], in_=r_twice[0], func=ACT.Square)
-        nc.vector.tensor_tensor(out=y[:, :, VH:V], in0=r_twice[1], in1=r_twice[1], op=ALU.mult)
-        gated = [keep.tile([P, S // 2], F32, name=f"gated{h}") for h in range(2)]
-        for h in range(2):
-            nc.vector.tensor_tensor(out=gated[h][:], in0=y[:].rearrange("p q v -> p (q v)"), in1=gates[h][:], op=ALU.mult)
-        for h in range(2):
-            nc.vector.tensor_copy(result[:].indirect(offsets[:, 32 * h : 32 * (h + 1)]), gated[h][:])
-        nc.sync.dma_start(out=out, in_=result[:])
+        halves = [slice(0, VH), slice(VH, V)]
+        for h in (0, 1):
+            nc.scalar.activation(out=r[:, halves[h]], in_=acc[h][:], func=ACT.Relu, bias=bias[:, 0:1])
+        for h in (1, 0):
+            nc.vector.scalar_tensor_tensor(
+                out=ug[:, halves[h]], in0=acc[h][:], scalar=bias[:, 0:1], in1=gates[:, halves[h]], op0=ALU.add, op1=ALU.mult
+            )
+        nc.scalar.activation(out=y[:], in_=r[:].unsqueeze(1).to_broadcast([P, D - 1, V]), func=ACT.Square)
+        nc.vector.tensor_tensor(result[:].indirect(offsets[:, 0 : V // 16]), r[:], ug[:], ALU.mult)
+        nc.vector.tensor_tensor(
+            result[:].indirect(offsets[:, V // 16 : S // 16]), y[:].rearrange("p d v -> p (d v)"), gates[:, V:S], ALU.mult
+        )
+        nc.sync.dma_start(out=out, in_=result[:, 0:T])

@@ -23,9 +23,9 @@ X_WINDOW = 1408
 OUT_WINDOW = 2048
 VH = V // 2
 
-X_VECTOR = ((192, 320), (0, 256), (320, 192), (64, 64))
-W_ENGINES = ("SSSS", "SSSS", "VSSS", "SVSB")
-X_SPLIT = ((512, 512), (512, 512), (1024,), (512, 512))
+X_VECTOR = ((256, 320), (64, 384), (192, 128), (0, 128))
+W_ENGINES = ("VSSS", "SSSS", "SSVS", "SSBB")
+X_SPLIT = ((1024,), (1024,), (1024,), (512, 512))
 W3_GROUPS = [(0, 1), (2,), (3,)]
 
 

from contextlib import ExitStack

import concourse.mybir as mybir

K, T, D, S, V, N = 2048, 1024, 4, 1024, 256, 128
FLOPS = 2 * N * S * K

F32 = mybir.dt.float32
BF16 = mybir.dt.bfloat16
U32 = mybir.dt.uint32
U16 = mybir.dt.uint16
U8 = mybir.dt.uint8
FP8X4 = mybir.dt.float8_e4m3fn_x4
ACT = mybir.ActivationFunctionType
ALU = mybir.AluOpType

P = 128
PACK = 4
PASS_K = P * PACK
PASSES = K // PASS_K
HALF = T // 2
X_WINDOW = 1408
OUT_WINDOW = 2048
VH = V // 2

X_VECTOR = ((256, 320), (64, 384), (192, 128), (0, 128))
W_ENGINES = ("VSSS", "SSSS", "SSVS", "SSBB")
X_SPLIT = ((1024,), (1024,), (1024,), (512, 512))
W3_GROUPS = [(0, 1), (2,), (3,)]


def tile_picked_tome_lin_relu2_sub_e_kernel(tc, xT, w, b, gate, offs, out):
    nc = tc.nc
    with ExitStack() as ctx:
        keep = ctx.enter_context(tc.tile_pool(name="keep", bufs=1))
        psum = ctx.enter_context(tc.psum_pool(name="psum", bufs=1))

        offsets = keep.tile([P, S // 16], U16, name="offsets")
        bias = keep.tile([P, 1], F32, name="bias")
        gates = keep.tile([P, S], F32, name="gates")
        x_raw = [[keep.tile([P, PACK, n], F32, name=f"x_raw{a}_{i}") for i, n in enumerate(X_SPLIT[a])] for a in range(PASSES)]
        w_groups = [[(0, 1, 2, 3)]] * 3 + [W3_GROUPS]
        w_raw = [[keep.tile([P, len(g), PACK, N], F32, name=f"w_raw{a}_{i}") for i, g in enumerate(w_groups[a])] for a in range(PASSES)]
        x_bf = [[keep.tile([P, HALF, PACK], BF16, name=f"x_bf{a}_{c}", align_bytes=64) for c in range(2)] for a in range(PASSES)]
        w_bf = [keep.tile([P, D, N, PACK], BF16, name=f"w_bf{a}", tag=f"ring{a}", align_bytes=64) for a in range(PASSES)]
        x_codes = [keep.tile([P, X_WINDOW], U32, name=f"x_codes{a}", align_bytes=64) for a in range(PASSES)]
        x_scales = keep.tile([P, X_WINDOW], U8, name="x_scales", align_bytes=64)
        picked_codes = [keep.tile([P, S], U32, name=f"picked_codes{a}", align_bytes=64) for a in range(PASSES - 1)]
        picked_scales = keep.tile([P, S], U8, name="picked_scales", align_bytes=64)
        w_codes = [keep.tile([P, D * N], U32, name=f"w_codes{a}", align_bytes=64) for a in range(PASSES)]
        w_scales = [keep.tile([P, D * N], U8, name=f"w_scales{a}", align_bytes=64) for a in range(PASSES)]
        r = keep.tile([P, V], F32, name="r")
        ug = keep.tile([P, V], F32, name="ug")
        y = keep.tile([P, D - 1, V], F32, name="y")
        result = keep.tile([P, OUT_WINDOW], F32, name="result")
        acc = [psum.tile([P, VH], F32, name=f"acc{h}") for h in range(2)]

        nc.scalar.dma_start(out=bias[:], in_=b)
        for a in range(PASSES):
            t0 = 0
            for i, n in enumerate(X_SPLIT[a]):
                src = xT[a * PASS_K : (a + 1) * PASS_K, t0 : t0 + n]
                nc.sync.dma_start(out=x_raw[a][i][:], in_=src.rearrange("(p j) t -> p j t", j=PACK))
                t0 += n
            if a == 0:
                nc.sync.dma_start(offsets[:], offs)
        for a in range(PASSES):
            for i, g in enumerate(w_groups[a]):
                src = w[g[0] : g[-1] + 1, a * PASS_K : (a + 1) * PASS_K, :].rearrange("d (p j) m -> p d j m", j=PACK)
                nc.sync.dma_start(out=w_raw[a][i][:], in_=src)
        nc.sync.dma_start(out=gates[:], in_=gate)

        nc.gpsimd.memset(x_scales[:], 0)
        for a in range(PASSES):
            nc.gpsimd.memset(x_codes[a][:, T:X_WINDOW], 0)

        def interleave(engine, dst, src):
            o = dst.rearrange("p (c i) j -> p c j i", i=4)
            s = src.rearrange("p j (c i) -> p c j i", i=4)
            if engine == "V":
                nc.vector.tensor_copy(out=o, in_=s)
            else:
                nc.scalar.copy(out=o, in_=s)

        def x_columns(a, lo, hi):
            t0 = 0
            for i, n in enumerate(X_SPLIT[a]):
                if t0 <= lo and hi <= t0 + n:
                    return x_raw[a][i][:, :, lo - t0 : hi - t0]
                t0 += n

        def convert_x(a, c):
            lo, mid, hi = c * HALF, (c + 1) * HALF - X_VECTOR[a][c], (c + 1) * HALF
            if mid > lo:
                interleave("S", x_bf[a][c][:, 0 : mid - lo, :], x_columns(a, lo, mid))
            if hi > mid:
                interleave("V", x_bf[a][c][:, mid - lo : HALF, :], x_columns(a, mid, hi))

        def quantize_x(a, c):
            cols = slice(c * HALF, (c + 1) * HALF)
            nc.vector.quantize_mx(
                out=x_codes[a][:, cols].bitcast(FP8X4),
                scales=x_scales[4 * a : P, cols],
                in_=x_bf[a][c][:].rearrange("p t j -> p (t j)"),
            )

        def convert_w(a, i):
            for n, d in enumerate(w_groups[a][i]):
                e = W_ENGINES[a][d]
                if e == "B":
                    interleave("S", w_bf[a][:, d, 0 : N // 2, :], w_raw[a][i][:, n, :, 0 : N // 2])
                    interleave("V", w_bf[a][:, d, N // 2 : N, :], w_raw[a][i][:, n, :, N // 2 : N])
                else:
                    interleave(e, w_bf[a][:, d, :, :], w_raw[a][i][:, n, :, :])

        def quantize_w(a, i):
            g = w_groups[a][i]
            cols = slice(g[0] * N, (g[-1] + 1) * N)
            nc.vector.quantize_mx(
                out=w_codes[a][:, cols].bitcast(FP8X4),
                scales=w_scales[a][:, cols],
                in_=w_bf[a][:, g[0] : g[-1] + 1, :, :].rearrange("p d m j -> p (d m j)"),
            )

        def gather(dst, src, lo, hi):
            nc.vector.tensor_copy(dst, src[:].indirect(offsets[:, lo // 16 : hi // 16]))

        def multiply(a, d):
            for h in range(2):
                cols = slice(d * V + h * VH, d * V + (h + 1) * VH)
                if a < PASSES - 1:
                    codes = picked_codes[a][:, cols]
                else:
                    codes = last_codes[d // 2][:, cols.start % (S // 2) : cols.start % (S // 2) + VH]
                nc.tensor.matmul_mx(
                    out=acc[h][:],
                    lhsT=w_codes[a][:, d * N : (d + 1) * N].bitcast(FP8X4),
                    lhsT_scale=w_scales[a][:, d * N : (d + 1) * N],
                    rhs=codes.bitcast(FP8X4),
                    rhs_scale=picked_scales[4 * a : P, cols],
                    start=(a == 0 and d == 0),
                    stop=(a == PASSES - 1 and d == D - 1),
                )

        def weights(a, i):
            convert_w(a, i)
            quantize_w(a, i)

        for a in range(PASSES):
            for c in range(2):
                convert_x(a, c)
            for c in range(2):
                quantize_x(a, c)
            if a < PASSES - 1:
                gather(picked_codes[a][:], x_codes[a], 0, S)
        gather(picked_scales[:, 0 : S // 2], x_scales, 0, S // 2)
        weights(0, 0)
        gather(picked_scales[:, S // 2 : S], x_scales, S // 2, S)
        for d in (0, 1):
            multiply(0, d)
        last_codes = []
        last_codes.append(keep.tile([P, S // 2], U32, name="last_codes0", tag="ring0", align_bytes=64))
        gather(last_codes[0][:], x_codes[3], 0, S // 2)
        weights(1, 0)
        for d in (0, 1):
            multiply(1, d)
        for a in (0, 1):
            for d in (2, 3):
                multiply(a, d)
        last_codes.append(keep.tile([P, S // 2], U32, name="last_codes1", tag="ring1", align_bytes=64))
        gather(last_codes[1][:], x_codes[3], S // 2, S)
        weights(2, 0)
        for d in range(D):
            multiply(2, d)
        for i, g in enumerate(W3_GROUPS):
            weights(3, i)
            for d in g:
                multiply(3, d)

        halves = [slice(0, VH), slice(VH, V)]
        for h in (0, 1):
            nc.scalar.activation(out=r[:, halves[h]], in_=acc[h][:], func=ACT.Relu, bias=bias[:, 0:1])
        for h in (1, 0):
            nc.vector.scalar_tensor_tensor(
                out=ug[:, halves[h]], in0=acc[h][:], scalar=bias[:, 0:1], in1=gates[:, halves[h]], op0=ALU.add, op1=ALU.mult
            )
        nc.scalar.activation(out=y[:], in_=r[:].unsqueeze(1).to_broadcast([P, D - 1, V]), func=ACT.Square)
        nc.vector.tensor_tensor(result[:].indirect(offsets[:, 0 : V // 16]), r[:], ug[:], ALU.mult)
        nc.vector.tensor_tensor(
            result[:].indirect(offsets[:, V // 16 : S // 16]), y[:].rearrange("p d v -> p (d v)"), gates[:, V:S], ALU.mult
        )
        nc.sync.dma_start(out=out, in_=result[:, 0:T])
